import numpy as np
import ml_dtypes


def mxq(x, axis, fmt="e4m3"):
    dtype, down = {"e4m3": (ml_dtypes.float8_e4m3fn, 7), "e5m2": (ml_dtypes.float8_e5m2, 14)}[fmt]
    v = np.moveaxis(np.asarray(x, np.float32).astype(ml_dtypes.bfloat16).astype(np.float64), axis, -1)
    blocks = v.reshape(v.shape[:-1] + (-1, 32))
    amax = np.abs(blocks).max(-1, keepdims=True)
    byte = np.maximum(np.where(amax > 0, np.frexp(amax)[1] - 1 + 127, 0) - down, 1)
    scale = np.exp2(byte - 127.0)
    codes = (blocks / scale).astype(np.float32).astype(dtype).astype(np.float64)
    return np.moveaxis((codes * scale).reshape(v.shape), -1, axis)


WIDE = False


def mx_kscale(k):
    if not WIDE:
        return np.ones(k)
    levels = np.array([30, -30])
    if k % 512:
        return np.exp2(np.random.permutation(np.resize(levels, k // 32))).repeat(32)
    a = np.empty((k // 512, 16))
    for p in range(k // 512):
        a[p, :8] = np.random.permutation(np.resize(levels, 8))
        for g in range(8):
            far = levels[np.abs(levels - a[p, g]) >= 10]
            a[p, g + 8] = far[np.random.randint(len(far))]
    return np.exp2(a.ravel()).repeat(32)


def f64(x):
    return np.asarray(x).astype(np.float64)


def striped(idx):
    return np.tile(np.asarray(idx).reshape(-1, 16).T, (8, 1)).astype(np.uint16)


def unstriped(offs):
    return offs[:16].T.reshape(-1).astype(np.int64)


E2M1 = np.array([0.0, 0.5, 1.0, 1.5, 2.0, 3.0, 4.0, 6.0, -0.0, -0.5, -1.0, -1.5, -2.0, -3.0, -4.0, -6.0])


def pack_weight(w, fmt):
    k, n = w.shape
    w = f64(np.asarray(w, np.float32).astype(ml_dtypes.bfloat16)).reshape(k // 32, 32, n)
    amax = np.abs(w).max(1)
    if fmt == "e4m3":
        byte = np.frexp(amax)[1] - 1 + 127 - 7
    else:
        mant, ex = np.frexp(amax / 6.0)
        byte = np.where(mant > 0.5, ex, ex - 1) + 127
    byte = np.clip(np.where(amax > 0, byte, 1), 1, 254)
    scaled = (w * np.exp2(127.0 - byte)[:, None, :]).reshape(k, n).astype(np.float32)
    by_word = np.ascontiguousarray(scaled.reshape(k // 512, 128, 4, n).transpose(0, 1, 3, 2))
    if fmt == "e4m3":
        words = by_word.astype(ml_dtypes.float8_e4m3fn).view(np.uint8)
    else:
        c = by_word.astype(ml_dtypes.float4_e2m1fn).view(np.uint8) & 0xF
        words = (c[..., 0::2] | (c[..., 1::2] << 4)).reshape(k // 512, 128, 2 * n)
    return np.ascontiguousarray(words), np.ascontiguousarray(byte.astype(np.uint8).reshape(k // 512, 16, n))


def unpack_weight(words, scales, fmt):
    g, _, n = scales.shape
    words = np.ascontiguousarray(words).reshape(g, 128, n, -1)
    if fmt == "e4m3":
        vals = words.view(ml_dtypes.float8_e4m3fn).astype(np.float64)
    else:
        nib = np.empty((g, 128, n, 4), np.uint8)
        nib[..., 0::2] = words & 0xF
        nib[..., 1::2] = words >> 4
        vals = E2M1[nib]
    vals = vals * np.repeat(np.exp2(scales.astype(np.float64) - 127.0), 8, axis=1)[..., None]
    return vals.transpose(0, 1, 3, 2).reshape(g * 512, n)


K, F, T, Z, J, R, C, O, N, E = 512, 512, 1024, 1024, 256, 512, 512, 128, 256, 1024


def setup_inputs():
    n = np.random.standard_normal
    idx = np.random.permutation(T)[:J]
    idx2 = np.random.permutation(Z)[:J]
    idx3 = np.random.permutation(C)[:J]
    idx4 = np.random.permutation(C)[:O]
    idx5 = np.random.permutation(C)[:O]
    idx6 = np.random.permutation(J)[:O]
    idx7 = np.random.permutation(E)[:O]
    fk = mx_kscale(K)
    fr = mx_kscale(R)
    ff = mx_kscale(F)
    xtp = pack_weight(n((K, T)) / fk[:, None], "e2m1")
    wp = pack_weight(n((K, R)) * 1 / np.sqrt(K) * fk[:, None] * fr, "e4m3")
    xop = pack_weight(n((F, Z)) / ff[:, None], "e4m3")
    w2p = pack_weight(n((F, R)) * 1 / np.sqrt(F) * ff[:, None] * fr, "e2m1")
    wbp = pack_weight(n((R, N)) * 1 / np.sqrt(R) / fr[:, None], "e2m1")
    return {
        "xt_words": xtp[0],
        "xt_scales": xtp[1],
        "w_words": wp[0],
        "w_scales": wp[1],
        "xo_words": xop[0],
        "xo_scales": xop[1],
        "w2_words": w2p[0],
        "w2_scales": w2p[1],
        "wb_words": wbp[0],
        "wb_scales": wbp[1],
        "tz": (n((N, E))).astype(np.float32),
        "offs": striped(idx),
        "offs2": striped(idx2),
        "offs3": striped(idx3),
        "offs4": striped(idx4),
        "offs5": striped(idx5),
        "offs6": striped(idx6),
        "offs7": striped(idx7),
    }


def reference(xt_words, xt_scales, w_words, w_scales, xo_words, xo_scales, w2_words, w2_scales, wb_words, wb_scales, tz, offs, offs2, offs3, offs4, offs5, offs6, offs7):
    idx = unstriped(offs)
    idx2 = unstriped(offs2)
    idx3 = unstriped(offs3)
    idx4 = unstriped(offs4)
    idx5 = unstriped(offs5)
    idx6 = unstriped(offs6)
    idx7 = unstriped(offs7)
    xtu = unpack_weight(xt_words, xt_scales, "e2m1")
    wu = unpack_weight(w_words, w_scales, "e4m3")
    xou = unpack_weight(xo_words, xo_scales, "e4m3")
    w2u = unpack_weight(w2_words, w2_scales, "e2m1")
    wbu = unpack_weight(wb_words, wb_scales, "e2m1")
    xtidxg = xtu[:, idx]
    a = wu.T @ xtidxg
    xoidx2g = xou[:, idx2]
    b = w2u.T @ xoidx2g
    pw = np.zeros((R, C))
    pw[:, idx3] = a
    hid = np.maximum(pw[:, idx4], pw[:, idx5]) - b[:, idx6]
    hidq = mxq(hid, 0, "e5m2")
    p = wbu.T @ hidq
    y = p + f64(tz)[:, idx7]
    return y

@@ -1,0 +1,173 @@
+from contextlib import ExitStack
+
+import concourse.mybir as mybir
+
+F32 = mybir.dt.float32
+BF16 = mybir.dt.bfloat16
+I32 = mybir.dt.int32
+U32 = mybir.dt.uint32
+U16 = mybir.dt.uint16
+U8 = mybir.dt.uint8
+E4M3 = mybir.dt.float8_e4m3fn_x4
+E5M2 = mybir.dt.float8_e5m2_x4
+E2M1 = mybir.dt.float4_e2m1fn_x4
+ALU = mybir.AluOpType
+COPY = mybir.ActivationFunctionType.Copy
+
+P = 128
+K, T, Z, J, R, C, O, N, E = 512, 1024, 1024, 256, 512, 512, 128, 256, 1024
+PACK = 4
+FLOPS = 2 * (2 * K * R * J + R * N * O)
+
+
+def tile_list_readless_twotab_one_tabled_kernel(
+    tc, xt_words, xt_scales, w_words, w_scales, xo_words, xo_scales, w2_words, w2_scales, wb_words, wb_scales,
+    tz, offs, offs2, offs3, offs4, offs5, offs6, offs7, out,
+):
+    nc = tc.nc
+    with ExitStack() as ctx:
+        keep = ctx.enter_context(tc.tile_pool(name="keep", bufs=1))
+        psum = ctx.enter_context(tc.psum_pool(name="psum", bufs=1))
+
+        def tile(name, width, dtype):
+            return keep.tile([P, width], dtype, name=name, align_bytes=64)
+
+        def load_list(name, src):
+            dst = tile(name, src.shape[1], U16)
+            nc.sync.dma_start(dst[:], src)
+            return dst
+
+        def load_words(queue, name, src, width, dtype):
+            dst = tile(name, width, dtype)
+            queue.dma_start(dst[:].bitcast(I32), src.bitcast(I32))
+            return dst
+
+        def scale_plane(name, src):
+            dst = tile(name, src.shape[2], U8)
+            return dst
+
+        def load_scales(queue, dst, src, fill=True):
+            for q in range(4):
+                rows = src[0, 4 * q : 4 * q + 4, :].bitcast(I32)
+                if fill:
+                    queue.dma_start(dst[32 * q : 32 * q + 32, :].bitcast(I32),
+                                    rows.unsqueeze(0).broadcast_to([8, 4, rows.shape[1]]))
+                else:
+                    queue.dma_start(dst[32 * q : 32 * q + 4, :].bitcast(I32), rows)
+
+        def deal(engine_copy, name, src, dtype, run):
+            dst = tile(name, R, dtype)
+            engine_copy(
+                dst[:].rearrange("p (t c i) -> p c t i", t=PACK, i=run),
+                src[:].rearrange("p (c i t) -> p c t i", t=PACK, i=run),
+            )
+            return dst
+
+        xt_s = scale_plane("xt_s", xt_scales)
+        w_s = scale_plane("w_s", w_scales)
+        xo_s = scale_plane("xo_s", xo_scales)
+        w2_s = scale_plane("w2_s", w2_scales)
+        wb_s = scale_plane("wb_s", wb_scales)
+        l1 = load_list("l1", offs)
+        xt_w = load_words(nc.sync, "xt_w", xt_words[0], T, U16)
+        load_scales(nc.sync, xt_s, xt_scales)
+        w_w = load_words(nc.sync, "w_w", w_words[0].rearrange("p n t -> p (n t)"), R, U32)
+        load_scales(nc.sync, w_s, w_scales)
+        l2 = load_list("l2", offs2)
+        xo_w = load_words(nc.sync, "xo_w", xo_words[0].rearrange("p n t -> p (n t)"), Z, U32)
+        load_scales(nc.sync, xo_s, xo_scales)
+        l3 = load_list("l3", offs3)
+        w2_w = load_words(nc.sync, "w2_w", w2_words[0], R, U16)
+        load_scales(nc.gpsimd, w2_s, w2_scales)
+        l4 = load_list("l4", offs4)
+        l5 = load_list("l5", offs5)
+        l6 = load_list("l6", offs6)
+        load_scales(nc.gpsimd, wb_s, wb_scales, False)
+        wb_w = load_words(nc.gpsimd, "wb_w", wb_words[0], N, U16)
+        l7 = load_list("l7", offs7)
+        tz_t = tile("tz_t", 2 * E, F32)
+        nc.sync.dma_start(tz_t[:].rearrange("p (h e) -> p h e", h=2), tz.rearrange("(h p) e -> p h e", h=2))
+
+        board = [tile("board%d" % t, C, F32) for t in range(PACK)]
+        for t in range(PACK):
+            nc.vector.memset(board[t][:], 0.0)
+
+        xt_gw = tile("xt_gw", J, U16)
+        xt_gs = tile("xt_gs", J, U8)
+        nc.vector.tensor_copy(xt_gw[:], xt_w[:].indirect(l1[:]))
+        nc.vector.tensor_copy(xt_gs[:], xt_s[:].indirect(l1[:]))
+        w_dw = deal(nc.scalar.copy, "w_dw", w_w, U32, 4)
+        w_ds = deal(nc.vector.tensor_copy, "w_ds", w_s, U8, 16)
+
+        a_ps = [psum.tile([P, J], F32, name="a_ps%d" % t) for t in range(PACK)]
+        for t in range(PACK):
+            cols = slice(t * P, (t + 1) * P)
+            nc.tensor.matmul_mx(a_ps[t][:], lhsT=w_dw[:, cols].bitcast(E4M3), lhsT_scale=w_ds[:, cols],
+                                rhs=xt_gw[:].bitcast(E2M1), rhs_scale=xt_gs[:], start=True, stop=True)
+
+        xo_gw = tile("xo_gw", J, U32)
+        xo_gs = tile("xo_gs", J, U8)
+        nc.vector.tensor_copy(xo_gw[:], xo_w[:].indirect(l2[:]))
+        nc.vector.tensor_copy(xo_gs[:], xo_s[:].indirect(l2[:]))
+        w2_dw = deal(nc.scalar.copy, "w2_dw", w2_w, U16, 8)
+        w2_ds = deal(nc.vector.tensor_copy, "w2_ds", w2_s, U8, 16)
+
+        b_ps = [psum.tile([P, 2 * J], F32, name="b_ps%d" % u) for u in range(2)]
+        for t in range(PACK):
+            cols = slice(t * P, (t + 1) * P)
+            nc.tensor.matmul_mx(b_ps[t // 2][:, (t % 2) * J : (t % 2 + 1) * J], lhsT=w2_dw[:, cols].bitcast(E2M1),
+                                lhsT_scale=w2_ds[:, cols], rhs=xo_gw[:].bitcast(E4M3), rhs_scale=xo_gs[:],
+                                start=True, stop=True)
+
+        def s_move(dst, src):
+            nc.scalar.activation(dst, src, COPY)
+
+        v_move = nc.vector.tensor_copy
+        a_sb = [tile("a_sb%d" % t, J, F32) for t in range(PACK)]
+        for t in (0, 2, 1, 3):
+            move = s_move if t < 2 else v_move
+            move(a_sb[t][:], a_ps[t][:])
+            move(board[t][:].indirect(l3[:]), a_sb[t][:])
+
+        first = [tile("first%d" % u, 2 * O, F32) for u in range(2)]
+        second = [tile("second%d" % u, 2 * O, F32) for u in range(2)]
+        for t in range(PACK):
+            move = s_move if t < 2 else v_move
+            cols = slice((t % 2) * O, (t % 2 + 1) * O)
+            move(first[t // 2][:, cols], board[t][:].indirect(l4[:]))
+            move(second[t // 2][:, cols], board[t][:].indirect(l5[:]))
+
+        b_sb = [tile("b_sb%d" % u, 2 * J, F32) for u in range(2)]
+        b_g = tile("b_g", PACK * O, F32)
+        for u in range(2):
+            s_move(b_sb[u][:], b_ps[u][:])
+        for t in range(PACK):
+            move = s_move if t < 3 else v_move
+            move(b_g[:, t * O : (t + 1) * O], b_sb[t // 2][:, (t % 2) * J : (t % 2 + 1) * J].indirect(l6[:]))
+
+        larger = tile("larger", PACK * O, F32)
+        for u in range(2):
+            nc.vector.tensor_tensor(larger[:, u * 2 * O : (u + 1) * 2 * O], first[u][:], second[u][:], ALU.max)
+        hid = tile("hid", PACK * O, BF16)
+        nc.vector.tensor_tensor(
+            hid[:].rearrange("p (c i t) -> p c t i", t=PACK, i=4),
+            larger[:].rearrange("p (t c i) -> p c t i", t=PACK, i=4),
+            b_g[:].rearrange("p (t c i) -> p c t i", t=PACK, i=4),
+            ALU.subtract,
+        )
+        hid_w = tile("hid_w", O, U32)
+        hid_s = tile("hid_s", O, U8)
+        nc.vector.quantize_mx(hid_w[:].bitcast(E5M2), hid_s[:], hid[:])
+
+        tz_g = tile("tz_g", 2 * O, F32)
+        for h in range(2):
+            s_move(tz_g[:, h * O : (h + 1) * O], tz_t[:, h * E : (h + 1) * E].indirect(l7[:]))
+
+        p_ps = psum.tile([P, 2 * O], F32, name="p_ps")
+        for h in range(2):
+            cols = slice(h * P, (h + 1) * P)
+            nc.tensor.matmul_mx(p_ps[:, h * O : (h + 1) * O], lhsT=wb_w[:, cols].bitcast(E2M1), lhsT_scale=wb_s[:, cols],
+                                rhs=hid_w[:].bitcast(E5M2), rhs_scale=hid_s[:], start=True, stop=True)
+        res = tile("res", 2 * O, F32)
+        nc.vector.tensor_tensor(res[:], p_ps[:], tz_g[:], ALU.add)
+        nc.sync.dma_start(out.rearrange("(h p) o -> p h o", h=2), res[:].rearrange("p (h o) -> p h o", h=2))

@@ -29,8 +29,8 @@ def tile_list_readless_twotab_one_tabled_kernel(
         keep = ctx.enter_context(tc.tile_pool(name="keep", bufs=1))
         psum = ctx.enter_context(tc.psum_pool(name="psum", bufs=1))
 
-        def tile(name, width, dtype):
-            return keep.tile([P, width], dtype, name=name, align_bytes=64)
+        def tile(name, width, dtype, tag=None):
+            return keep.tile([P, width], dtype, name=name, tag=tag or name, align_bytes=64)
 
         def load_list(name, src):
             dst = tile(name, src.shape[1], U16)
@@ -46,8 +46,8 @@ def tile_list_readless_twotab_one_tabled_kernel(
             dst = tile(name, src.shape[2], U8)
             return dst
 
-        def load_scales(queue, dst, src, fill=True):
-            for q in range(4):
+        def load_scales(queue, dst, src, fill=True, quads=(0, 1, 2, 3)):
+            for q in quads:
                 rows = src[0, 4 * q : 4 * q + 4, :].bitcast(I32)
                 if fill:
                     queue.dma_start(dst[32 * q : 32 * q + 32, :].bitcast(I32),
@@ -69,24 +69,24 @@ def tile_list_readless_twotab_one_tabled_kernel(
         w2_s = scale_plane("w2_s", w2_scales)
         wb_s = scale_plane("wb_s", wb_scales)
         l1 = load_list("l1", offs)
-        xt_w = load_words(nc.sync, "xt_w", xt_words[0], T, U16)
         load_scales(nc.sync, xt_s, xt_scales)
+        xt_w = load_words(nc.sync, "xt_w", xt_words[0], T, U16)
         w_w = load_words(nc.sync, "w_w", w_words[0].rearrange("p n t -> p (n t)"), R, U32)
         load_scales(nc.sync, w_s, w_scales)
-        l2 = load_list("l2", offs2)
-        xo_w = load_words(nc.sync, "xo_w", xo_words[0].rearrange("p n t -> p (n t)"), Z, U32)
-        load_scales(nc.sync, xo_s, xo_scales)
         l3 = load_list("l3", offs3)
+        xo_w = load_words(nc.sync, "xo_w", xo_words[0].rearrange("p n t -> p (n t)"), Z, U32)
+        l2 = load_list("l2", offs2)
+        load_scales(nc.sync, xo_s, xo_scales)
         w2_w = load_words(nc.sync, "w2_w", w2_words[0], R, U16)
-        load_scales(nc.gpsimd, w2_s, w2_scales)
         l4 = load_list("l4", offs4)
         l5 = load_list("l5", offs5)
+        load_scales(nc.sync, w2_s, w2_scales)
         l6 = load_list("l6", offs6)
-        load_scales(nc.gpsimd, wb_s, wb_scales, False)
-        wb_w = load_words(nc.gpsimd, "wb_w", wb_words[0], N, U16)
+        wb_w = load_words(nc.sync, "wb_w", wb_words[0], N, U16)
         l7 = load_list("l7", offs7)
         tz_t = tile("tz_t", 2 * E, F32)
         nc.sync.dma_start(tz_t[:].rearrange("p (h e) -> p h e", h=2), tz.rearrange("(h p) e -> p h e", h=2))
+        load_scales(nc.sync, wb_s, wb_scales, False)
 
         board = [tile("board%d" % t, C, F32) for t in range(PACK)]
         for t in range(PACK):
@@ -94,13 +94,18 @@ def tile_list_readless_twotab_one_tabled_kernel(
 
         xt_gw = tile("xt_gw", J, U16)
         xt_gs = tile("xt_gs", J, U8)
-        nc.vector.tensor_copy(xt_gw[:], xt_w[:].indirect(l1[:]))
         nc.vector.tensor_copy(xt_gs[:], xt_s[:].indirect(l1[:]))
+        nc.vector.tensor_copy(xt_gw[:], xt_w[:].indirect(l1[:]))
         w_dw = deal(nc.scalar.copy, "w_dw", w_w, U32, 4)
-        w_ds = deal(nc.vector.tensor_copy, "w_ds", w_s, U8, 16)
+        w_ds = tile("w_ds", R, U8)
+        for u in range(2):
+            nc.vector.tensor_copy(
+                w_ds[:].rearrange("p (t c i) -> p c t i", t=PACK, i=16)[:, :, u::2, :],
+                w_s[:].rearrange("p (c i t) -> p c t i", t=PACK, i=16)[:, :, u::2, :],
+            )
 
         a_ps = [psum.tile([P, J], F32, name="a_ps%d" % t) for t in range(PACK)]
-        for t in range(PACK):
+        for t in (2, 0, 1, 3):
             cols = slice(t * P, (t + 1) * P)
             nc.tensor.matmul_mx(a_ps[t][:], lhsT=w_dw[:, cols].bitcast(E4M3), lhsT_scale=w_ds[:, cols],
                                 rhs=xt_gw[:].bitcast(E2M1), rhs_scale=xt_gs[:], start=True, stop=True)
@@ -109,8 +114,12 @@ def tile_list_readless_twotab_one_tabled_kernel(
         xo_gs = tile("xo_gs", J, U8)
         nc.vector.tensor_copy(xo_gw[:], xo_w[:].indirect(l2[:]))
         nc.vector.tensor_copy(xo_gs[:], xo_s[:].indirect(l2[:]))
-        w2_dw = deal(nc.scalar.copy, "w2_dw", w2_w, U16, 8)
-        w2_ds = deal(nc.vector.tensor_copy, "w2_ds", w2_s, U8, 16)
+        w2_dw = tile("w2_dw", R, U16)
+        nc.gpsimd.tensor_copy(
+            w2_dw[:].bitcast(U8).rearrange("p (t c i e) -> p c t i e", t=PACK, i=8, e=2),
+            w2_w[:].bitcast(U8).rearrange("p (c i t e) -> p c t i e", t=PACK, i=8, e=2),
+        )
+        w2_ds = deal(nc.gpsimd.tensor_copy, "w2_ds", w2_s, U8, 16)
 
         b_ps = [psum.tile([P, 2 * J], F32, name="b_ps%d" % u) for u in range(2)]
         for t in range(PACK):
@@ -123,11 +132,11 @@ def tile_list_readless_twotab_one_tabled_kernel(
             nc.scalar.activation(dst, src, COPY)
 
         v_move = nc.vector.tensor_copy
-        a_sb = [tile("a_sb%d" % t, J, F32) for t in range(PACK)]
-        for t in (0, 2, 1, 3):
+        for t in (2, 0, 1, 3):
             move = s_move if t < 2 else v_move
-            move(a_sb[t][:], a_ps[t][:])
-            move(board[t][:].indirect(l3[:]), a_sb[t][:])
+            a_sb = tile("a_sb%d" % t, J, F32, "xo_s" if t == 3 else None)
+            move(a_sb[:], a_ps[t][:])
+            move(board[t][:].indirect(l3[:]), a_sb[:])
 
         first = [tile("first%d" % u, 2 * O, F32) for u in range(2)]
         second = [tile("second%d" % u, 2 * O, F32) for u in range(2)]
@@ -159,15 +168,15 @@ def tile_list_readless_twotab_one_tabled_kernel(
         hid_s = tile("hid_s", O, U8)
         nc.vector.quantize_mx(hid_w[:].bitcast(E5M2), hid_s[:], hid[:])
 
-        tz_g = tile("tz_g", 2 * O, F32)
+        tz_g = tile("tz_g", 2 * O, F32, "b_sb1")
         for h in range(2):
             s_move(tz_g[:, h * O : (h + 1) * O], tz_t[:, h * E : (h + 1) * E].indirect(l7[:]))
 
-        p_ps = psum.tile([P, 2 * O], F32, name="p_ps")
         for h in range(2):
             cols = slice(h * P, (h + 1) * P)
-            nc.tensor.matmul_mx(p_ps[:, h * O : (h + 1) * O], lhsT=wb_w[:, cols].bitcast(E2M1), lhsT_scale=wb_s[:, cols],
+            p_ps = psum.tile([P, O], F32, name="p_ps%d" % h)
+            nc.tensor.matmul_mx(p_ps[:], lhsT=wb_w[:, cols].bitcast(E2M1), lhsT_scale=wb_s[:, cols],
                                 rhs=hid_w[:].bitcast(E5M2), rhs_scale=hid_s[:], start=True, stop=True)
-        res = tile("res", 2 * O, F32)
-        nc.vector.tensor_tensor(res[:], p_ps[:], tz_g[:], ALU.add)
-        nc.sync.dma_start(out.rearrange("(h p) o -> p h o", h=2), res[:].rearrange("p (h o) -> p h o", h=2))
+            res = tile("res%d" % h, O, F32)
+            nc.vector.tensor_tensor(res[:], p_ps[:], tz_g[:, h * O : (h + 1) * O], ALU.add)
+            nc.sync.dma_start(out[cols, :], res[:])

@@ -15,8 +15,12 @@ ALU = mybir.AluOpType
 COPY = mybir.ActivationFunctionType.Copy
 
 P = 128
-K, T, Z, J, R, C, O, N, E = 512, 1024, 1024, 256, 512, 512, 128, 256, 1024
 PACK = 4
+QUADRANT = 32
+LINE = 16
+K, T, Z, J, R, C, O, N, E = 512, 1024, 1024, 256, 512, 512, 128, 256, 1024
+SCALAR_SLICES = 2
+SLICE_ORDER = (2, 0, 1, 3)
 FLOPS = 2 * (2 * K * R * J + R * N * O)
 
 
@@ -29,64 +33,63 @@ def tile_list_readless_twotab_one_tabled_kernel(
         keep = ctx.enter_context(tc.tile_pool(name="keep", bufs=1))
         psum = ctx.enter_context(tc.psum_pool(name="psum", bufs=1))
 
-        def tile(name, width, dtype, tag=None):
-            return keep.tile([P, width], dtype, name=name, tag=tag or name, align_bytes=64)
+        def tile(name, width, dtype, on_bytes_of=None):
+            return keep.tile([P, width], dtype, name=name, tag=on_bytes_of or name, align_bytes=64)
 
         def load_list(name, src):
             dst = tile(name, src.shape[1], U16)
             nc.sync.dma_start(dst[:], src)
             return dst
 
-        def load_words(queue, name, src, width, dtype):
+        def load_words(name, src, width, dtype):
             dst = tile(name, width, dtype)
-            queue.dma_start(dst[:].bitcast(I32), src.bitcast(I32))
+            nc.sync.dma_start(dst[:].bitcast(I32), src.bitcast(I32))
             return dst
 
-        def scale_plane(name, src):
-            dst = tile(name, src.shape[2], U8)
-            return dst
+        def scale_rows(src, q):
+            return src[0, 4 * q : 4 * q + 4, :].bitcast(I32)
 
-        def load_scales(queue, dst, src, fill=True, quads=(0, 1, 2, 3)):
-            for q in quads:
-                rows = src[0, 4 * q : 4 * q + 4, :].bitcast(I32)
-                if fill:
-                    queue.dma_start(dst[32 * q : 32 * q + 32, :].bitcast(I32),
-                                    rows.unsqueeze(0).broadcast_to([8, 4, rows.shape[1]]))
-                else:
-                    queue.dma_start(dst[32 * q : 32 * q + 4, :].bitcast(I32), rows)
+        def load_scales_filled(dst, src, quadrants):
+            for q in quadrants:
+                rows = scale_rows(src, q)
+                nc.sync.dma_start(dst[QUADRANT * q : QUADRANT * (q + 1), :].bitcast(I32),
+                                  rows.unsqueeze(0).broadcast_to([QUADRANT // 4, 4, rows.shape[1]]))
 
-        def deal(engine_copy, name, src, dtype, run):
-            dst = tile(name, R, dtype)
-            engine_copy(
-                dst[:].rearrange("p (t c i) -> p c t i", t=PACK, i=run),
-                src[:].rearrange("p (c i t) -> p c t i", t=PACK, i=run),
-            )
-            return dst
+        def dealt(ap, run):
+            return ap.rearrange("p (t c i) -> p c t i", t=PACK, i=run)
 
-        xt_s = scale_plane("xt_s", xt_scales)
-        w_s = scale_plane("w_s", w_scales)
-        xo_s = scale_plane("xo_s", xo_scales)
-        w2_s = scale_plane("w2_s", w2_scales)
-        wb_s = scale_plane("wb_s", wb_scales)
-        l1 = load_list("l1", offs)
-        load_scales(nc.sync, xt_s, xt_scales)
-        xt_w = load_words(nc.sync, "xt_w", xt_words[0], T, U16)
-        w_w = load_words(nc.sync, "w_w", w_words[0].rearrange("p n t -> p (n t)"), R, U32)
-        load_scales(nc.sync, w_s, w_scales)
-        l3 = load_list("l3", offs3)
-        xo_w = load_words(nc.sync, "xo_w", xo_words[0].rearrange("p n t -> p (n t)"), Z, U32)
-        l2 = load_list("l2", offs2)
-        load_scales(nc.sync, xo_s, xo_scales)
-        w2_w = load_words(nc.sync, "w2_w", w2_words[0], R, U16)
-        l4 = load_list("l4", offs4)
-        l5 = load_list("l5", offs5)
-        load_scales(nc.sync, w2_s, w2_scales)
-        l6 = load_list("l6", offs6)
-        wb_w = load_words(nc.sync, "wb_w", wb_words[0], N, U16)
-        l7 = load_list("l7", offs7)
-        tz_t = tile("tz_t", 2 * E, F32)
-        nc.sync.dma_start(tz_t[:].rearrange("p (h e) -> p h e", h=2), tz.rearrange("(h p) e -> p h e", h=2))
-        load_scales(nc.sync, wb_s, wb_scales, False)
+        def undealt(ap, run):
+            return ap.rearrange("p (c i t) -> p c t i", t=PACK, i=run)
+
+        def scalar_move(dst, src):
+            nc.scalar.activation(dst, src, COPY)
+
+        def slice_move(t):
+            return scalar_move if t < SCALAR_SLICES else nc.vector.tensor_copy
+
+        xt_s, w_s, xo_s = tile("xt_s", T, U8), tile("w_s", R, U8), tile("xo_s", Z, U8)
+        w2_s, wb_s = tile("w2_s", R, U8), tile("wb_s", N, U8)
+        idx = load_list("idx", offs)
+        load_scales_filled(xt_s, xt_scales, range(4))
+        xt_w = load_words("xt_w", xt_words[0], T, U16)
+        w_w = load_words("w_w", w_words[0].rearrange("p n t -> p (n t)"), R, U32)
+        load_scales_filled(w_s, w_scales, range(4))
+        idx3 = load_list("idx3", offs3)
+        xo_w = load_words("xo_w", xo_words[0].rearrange("p n t -> p (n t)"), Z, U32)
+        idx2 = load_list("idx2", offs2)
+        load_scales_filled(xo_s, xo_scales, range(3))
+        w2_w = load_words("w2_w", w2_words[0], R, U16)
+        load_scales_filled(xo_s, xo_scales, range(3, 4))
+        idx4 = load_list("idx4", offs4)
+        idx5 = load_list("idx5", offs5)
+        load_scales_filled(w2_s, w2_scales, range(4))
+        idx6 = load_list("idx6", offs6)
+        wb_w = load_words("wb_w", wb_words[0], N, U16)
+        idx7 = load_list("idx7", offs7)
+        tz_sb = tile("tz_sb", 2 * E, F32)
+        nc.sync.dma_start(tz_sb[:].rearrange("p (h e) -> p h e", h=2), tz.rearrange("(h p) e -> p h e", h=2))
+        for q in range(4):
+            nc.sync.dma_start(wb_s[QUADRANT * q : QUADRANT * q + 4, :].bitcast(I32), scale_rows(wb_scales, q))
 
         board = [tile("board%d" % t, C, F32) for t in range(PACK)]
         for t in range(PACK):
@@ -94,33 +97,30 @@ def tile_list_readless_twotab_one_tabled_kernel(
 
         xt_gw = tile("xt_gw", J, U16)
         xt_gs = tile("xt_gs", J, U8)
-        nc.vector.tensor_copy(xt_gs[:], xt_s[:].indirect(l1[:]))
-        nc.vector.tensor_copy(xt_gw[:], xt_w[:].indirect(l1[:]))
-        w_dw = deal(nc.scalar.copy, "w_dw", w_w, U32, 4)
+        nc.vector.tensor_copy(xt_gs[:], xt_s[:].indirect(idx[:]))
+        nc.vector.tensor_copy(xt_gw[:], xt_w[:].indirect(idx[:]))
+        w_dw = tile("w_dw", R, U32)
+        nc.scalar.copy(dealt(w_dw[:], LINE // 4), undealt(w_w[:], LINE // 4))
         w_ds = tile("w_ds", R, U8)
-        for u in range(2):
-            nc.vector.tensor_copy(
-                w_ds[:].rearrange("p (t c i) -> p c t i", t=PACK, i=16)[:, :, u::2, :],
-                w_s[:].rearrange("p (c i t) -> p c t i", t=PACK, i=16)[:, :, u::2, :],
-            )
-
+        for parity in range(2):
+            nc.vector.tensor_copy(dealt(w_ds[:], LINE)[:, :, parity::2, :], undealt(w_s[:], LINE)[:, :, parity::2, :])
         a_ps = [psum.tile([P, J], F32, name="a_ps%d" % t) for t in range(PACK)]
-        for t in (2, 0, 1, 3):
+        for t in SLICE_ORDER:
             cols = slice(t * P, (t + 1) * P)
             nc.tensor.matmul_mx(a_ps[t][:], lhsT=w_dw[:, cols].bitcast(E4M3), lhsT_scale=w_ds[:, cols],
                                 rhs=xt_gw[:].bitcast(E2M1), rhs_scale=xt_gs[:], start=True, stop=True)
 
         xo_gw = tile("xo_gw", J, U32)
         xo_gs = tile("xo_gs", J, U8)
-        nc.vector.tensor_copy(xo_gw[:], xo_w[:].indirect(l2[:]))
-        nc.vector.tensor_copy(xo_gs[:], xo_s[:].indirect(l2[:]))
+        nc.vector.tensor_copy(xo_gw[:], xo_w[:].indirect(idx2[:]))
+        nc.vector.tensor_copy(xo_gs[:], xo_s[:].indirect(idx2[:]))
         w2_dw = tile("w2_dw", R, U16)
         nc.gpsimd.tensor_copy(
-            w2_dw[:].bitcast(U8).rearrange("p (t c i e) -> p c t i e", t=PACK, i=8, e=2),
-            w2_w[:].bitcast(U8).rearrange("p (c i t e) -> p c t i e", t=PACK, i=8, e=2),
+            w2_dw[:].bitcast(U8).rearrange("p (t c i e) -> p c t i e", t=PACK, i=LINE // 2, e=2),
+            w2_w[:].bitcast(U8).rearrange("p (c i t e) -> p c t i e", t=PACK, i=LINE // 2, e=2),
         )
-        w2_ds = deal(nc.gpsimd.tensor_copy, "w2_ds", w2_s, U8, 16)
-
+        w2_ds = tile("w2_ds", R, U8)
+        nc.gpsimd.tensor_copy(dealt(w2_ds[:], LINE), undealt(w2_s[:], LINE))
         b_ps = [psum.tile([P, 2 * J], F32, name="b_ps%d" % u) for u in range(2)]
         for t in range(PACK):
             cols = slice(t * P, (t + 1) * P)
@@ -128,55 +128,44 @@ def tile_list_readless_twotab_one_tabled_kernel(
                                 lhsT_scale=w2_ds[:, cols], rhs=xo_gw[:].bitcast(E4M3), rhs_scale=xo_gs[:],
                                 start=True, stop=True)
 
-        def s_move(dst, src):
-            nc.scalar.activation(dst, src, COPY)
+        for t in SLICE_ORDER:
+            a_sb = tile("a_sb%d" % t, J, F32, "xo_s" if t == SLICE_ORDER[-1] else None)
+            slice_move(t)(a_sb[:], a_ps[t][:])
+            slice_move(t)(board[t][:].indirect(idx3[:]), a_sb[:])
 
-        v_move = nc.vector.tensor_copy
-        for t in (2, 0, 1, 3):
-            move = s_move if t < 2 else v_move
-            a_sb = tile("a_sb%d" % t, J, F32, "xo_s" if t == 3 else None)
-            move(a_sb[:], a_ps[t][:])
-            move(board[t][:].indirect(l3[:]), a_sb[:])
-
-        first = [tile("first%d" % u, 2 * O, F32) for u in range(2)]
-        second = [tile("second%d" % u, 2 * O, F32) for u in range(2)]
+        by_idx4 = [tile("by_idx4_%d" % u, 2 * O, F32) for u in range(2)]
+        by_idx5 = [tile("by_idx5_%d" % u, 2 * O, F32) for u in range(2)]
         for t in range(PACK):
-            move = s_move if t < 2 else v_move
             cols = slice((t % 2) * O, (t % 2 + 1) * O)
-            move(first[t // 2][:, cols], board[t][:].indirect(l4[:]))
-            move(second[t // 2][:, cols], board[t][:].indirect(l5[:]))
+            slice_move(t)(by_idx4[t // 2][:, cols], board[t][:].indirect(idx4[:]))
+            slice_move(t)(by_idx5[t // 2][:, cols], board[t][:].indirect(idx5[:]))
 
         b_sb = [tile("b_sb%d" % u, 2 * J, F32) for u in range(2)]
         b_g = tile("b_g", PACK * O, F32)
         for u in range(2):
-            s_move(b_sb[u][:], b_ps[u][:])
+            scalar_move(b_sb[u][:], b_ps[u][:])
         for t in range(PACK):
-            move = s_move if t < 3 else v_move
-            move(b_g[:, t * O : (t + 1) * O], b_sb[t // 2][:, (t % 2) * J : (t % 2 + 1) * J].indirect(l6[:]))
+            scalar_move(b_g[:, t * O : (t + 1) * O], b_sb[t // 2][:, (t % 2) * J : (t % 2 + 1) * J].indirect(idx6[:]))
 
         larger = tile("larger", PACK * O, F32)
         for u in range(2):
-            nc.vector.tensor_tensor(larger[:, u * 2 * O : (u + 1) * 2 * O], first[u][:], second[u][:], ALU.max)
+            nc.vector.tensor_tensor(larger[:, u * 2 * O : (u + 1) * 2 * O], by_idx4[u][:], by_idx5[u][:], ALU.max)
         hid = tile("hid", PACK * O, BF16)
-        nc.vector.tensor_tensor(
-            hid[:].rearrange("p (c i t) -> p c t i", t=PACK, i=4),
-            larger[:].rearrange("p (t c i) -> p c t i", t=PACK, i=4),
-            b_g[:].rearrange("p (t c i) -> p c t i", t=PACK, i=4),
-            ALU.subtract,
-        )
+        nc.vector.tensor_tensor(undealt(hid[:], LINE // 4), dealt(larger[:], LINE // 4), dealt(b_g[:], LINE // 4),
+                                ALU.subtract)
         hid_w = tile("hid_w", O, U32)
         hid_s = tile("hid_s", O, U8)
         nc.vector.quantize_mx(hid_w[:].bitcast(E5M2), hid_s[:], hid[:])
 
         tz_g = tile("tz_g", 2 * O, F32, "b_sb1")
         for h in range(2):
-            s_move(tz_g[:, h * O : (h + 1) * O], tz_t[:, h * E : (h + 1) * E].indirect(l7[:]))
+            scalar_move(tz_g[:, h * O : (h + 1) * O], tz_sb[:, h * E : (h + 1) * E].indirect(idx7[:]))
 
         for h in range(2):
-            cols = slice(h * P, (h + 1) * P)
+            rows = slice(h * P, (h + 1) * P)
             p_ps = psum.tile([P, O], F32, name="p_ps%d" % h)
-            nc.tensor.matmul_mx(p_ps[:], lhsT=wb_w[:, cols].bitcast(E2M1), lhsT_scale=wb_s[:, cols],
+            nc.tensor.matmul_mx(p_ps[:], lhsT=wb_w[:, rows].bitcast(E2M1), lhsT_scale=wb_s[:, rows],
                                 rhs=hid_w[:].bitcast(E5M2), rhs_scale=hid_s[:], start=True, stop=True)
             res = tile("res%d" % h, O, F32)
             nc.vector.tensor_tensor(res[:], p_ps[:], tz_g[:, h * O : (h + 1) * O], ALU.add)
-            nc.sync.dma_start(out[cols, :], res[:])
+            nc.sync.dma_start(out[rows, :], res[:])

from contextlib import ExitStack

import concourse.mybir as mybir

F32 = mybir.dt.float32
BF16 = mybir.dt.bfloat16
I32 = mybir.dt.int32
U32 = mybir.dt.uint32
U16 = mybir.dt.uint16
U8 = mybir.dt.uint8
E4M3 = mybir.dt.float8_e4m3fn_x4
E5M2 = mybir.dt.float8_e5m2_x4
E2M1 = mybir.dt.float4_e2m1fn_x4
ALU = mybir.AluOpType
COPY = mybir.ActivationFunctionType.Copy

P = 128
PACK = 4
QUADRANT = 32
LINE = 16
K, T, Z, J, R, C, O, N, E = 512, 1024, 1024, 256, 512, 512, 128, 256, 1024
SCALAR_SLICES = 2
SLICE_ORDER = (2, 0, 1, 3)
FLOPS = 2 * (2 * K * R * J + R * N * O)


def tile_list_readless_twotab_one_tabled_kernel(
    tc, xt_words, xt_scales, w_words, w_scales, xo_words, xo_scales, w2_words, w2_scales, wb_words, wb_scales,
    tz, offs, offs2, offs3, offs4, offs5, offs6, offs7, out,
):
    nc = tc.nc
    with ExitStack() as ctx:
        keep = ctx.enter_context(tc.tile_pool(name="keep", bufs=1))
        psum = ctx.enter_context(tc.psum_pool(name="psum", bufs=1))

        def tile(name, width, dtype, on_bytes_of=None):
            return keep.tile([P, width], dtype, name=name, tag=on_bytes_of or name, align_bytes=64)

        def load_list(name, src):
            dst = tile(name, src.shape[1], U16)
            nc.sync.dma_start(dst[:], src)
            return dst

        def load_words(name, src, width, dtype):
            dst = tile(name, width, dtype)
            nc.sync.dma_start(dst[:].bitcast(I32), src.bitcast(I32))
            return dst

        def scale_rows(src, q):
            return src[0, 4 * q : 4 * q + 4, :].bitcast(I32)

        def load_scales_filled(dst, src, quadrants):
            for q in quadrants:
                rows = scale_rows(src, q)
                nc.sync.dma_start(dst[QUADRANT * q : QUADRANT * (q + 1), :].bitcast(I32),
                                  rows.unsqueeze(0).broadcast_to([QUADRANT // 4, 4, rows.shape[1]]))

        def dealt(ap, run):
            return ap.rearrange("p (t c i) -> p c t i", t=PACK, i=run)

        def undealt(ap, run):
            return ap.rearrange("p (c i t) -> p c t i", t=PACK, i=run)

        def scalar_move(dst, src):
            nc.scalar.activation(dst, src, COPY)

        def slice_move(t):
            return scalar_move if t < SCALAR_SLICES else nc.vector.tensor_copy

        xt_s, w_s, xo_s = tile("xt_s", T, U8), tile("w_s", R, U8), tile("xo_s", Z, U8)
        w2_s, wb_s = tile("w2_s", R, U8), tile("wb_s", N, U8)
        idx = load_list("idx", offs)
        load_scales_filled(xt_s, xt_scales, range(4))
        xt_w = load_words("xt_w", xt_words[0], T, U16)
        w_w = load_words("w_w", w_words[0].rearrange("p n t -> p (n t)"), R, U32)
        load_scales_filled(w_s, w_scales, range(4))
        idx3 = load_list("idx3", offs3)
        xo_w = load_words("xo_w", xo_words[0].rearrange("p n t -> p (n t)"), Z, U32)
        idx2 = load_list("idx2", offs2)
        load_scales_filled(xo_s, xo_scales, range(3))
        w2_w = load_words("w2_w", w2_words[0], R, U16)
        load_scales_filled(xo_s, xo_scales, range(3, 4))
        idx4 = load_list("idx4", offs4)
        idx5 = load_list("idx5", offs5)
        load_scales_filled(w2_s, w2_scales, range(4))
        idx6 = load_list("idx6", offs6)
        wb_w = load_words("wb_w", wb_words[0], N, U16)
        idx7 = load_list("idx7", offs7)
        tz_sb = tile("tz_sb", 2 * E, F32)
        nc.sync.dma_start(tz_sb[:].rearrange("p (h e) -> p h e", h=2), tz.rearrange("(h p) e -> p h e", h=2))
        for q in range(4):
            nc.sync.dma_start(wb_s[QUADRANT * q : QUADRANT * q + 4, :].bitcast(I32), scale_rows(wb_scales, q))

        board = [tile("board%d" % t, C, F32) for t in range(PACK)]
        for t in range(PACK):
            nc.vector.memset(board[t][:], 0.0)

        xt_gw = tile("xt_gw", J, U16)
        xt_gs = tile("xt_gs", J, U8)
        nc.vector.tensor_copy(xt_gs[:], xt_s[:].indirect(idx[:]))
        nc.vector.tensor_copy(xt_gw[:], xt_w[:].indirect(idx[:]))
        w_dw = tile("w_dw", R, U32)
        nc.scalar.copy(dealt(w_dw[:], LINE // 4), undealt(w_w[:], LINE // 4))
        w_ds = tile("w_ds", R, U8)
        for parity in range(2):
            nc.vector.tensor_copy(dealt(w_ds[:], LINE)[:, :, parity::2, :], undealt(w_s[:], LINE)[:, :, parity::2, :])
        a_ps = [psum.tile([P, J], F32, name="a_ps%d" % t) for t in range(PACK)]
        for t in SLICE_ORDER:
            cols = slice(t * P, (t + 1) * P)
            nc.tensor.matmul_mx(a_ps[t][:], lhsT=w_dw[:, cols].bitcast(E4M3), lhsT_scale=w_ds[:, cols],
                                rhs=xt_gw[:].bitcast(E2M1), rhs_scale=xt_gs[:], start=True, stop=True)

        xo_gw = tile("xo_gw", J, U32)
        xo_gs = tile("xo_gs", J, U8)
        nc.vector.tensor_copy(xo_gw[:], xo_w[:].indirect(idx2[:]))
        nc.vector.tensor_copy(xo_gs[:], xo_s[:].indirect(idx2[:]))
        w2_dw = tile("w2_dw", R, U16)
        nc.gpsimd.tensor_copy(
            w2_dw[:].bitcast(U8).rearrange("p (t c i e) -> p c t i e", t=PACK, i=LINE // 2, e=2),
            w2_w[:].bitcast(U8).rearrange("p (c i t e) -> p c t i e", t=PACK, i=LINE // 2, e=2),
        )
        w2_ds = tile("w2_ds", R, U8)
        nc.gpsimd.tensor_copy(dealt(w2_ds[:], LINE), undealt(w2_s[:], LINE))
        b_ps = [psum.tile([P, 2 * J], F32, name="b_ps%d" % u) for u in range(2)]
        for t in range(PACK):
            cols = slice(t * P, (t + 1) * P)
            nc.tensor.matmul_mx(b_ps[t // 2][:, (t % 2) * J : (t % 2 + 1) * J], lhsT=w2_dw[:, cols].bitcast(E2M1),
                                lhsT_scale=w2_ds[:, cols], rhs=xo_gw[:].bitcast(E4M3), rhs_scale=xo_gs[:],
                                start=True, stop=True)

        for t in SLICE_ORDER:
            a_sb = tile("a_sb%d" % t, J, F32, "xo_s" if t == SLICE_ORDER[-1] else None)
            slice_move(t)(a_sb[:], a_ps[t][:])
            slice_move(t)(board[t][:].indirect(idx3[:]), a_sb[:])

        by_idx4 = [tile("by_idx4_%d" % u, 2 * O, F32) for u in range(2)]
        by_idx5 = [tile("by_idx5_%d" % u, 2 * O, F32) for u in range(2)]
        for t in range(PACK):
            cols = slice((t % 2) * O, (t % 2 + 1) * O)
            slice_move(t)(by_idx4[t // 2][:, cols], board[t][:].indirect(idx4[:]))
            slice_move(t)(by_idx5[t // 2][:, cols], board[t][:].indirect(idx5[:]))

        b_sb = [tile("b_sb%d" % u, 2 * J, F32) for u in range(2)]
        b_g = tile("b_g", PACK * O, F32)
        for u in range(2):
            scalar_move(b_sb[u][:], b_ps[u][:])
        for t in range(PACK):
            scalar_move(b_g[:, t * O : (t + 1) * O], b_sb[t // 2][:, (t % 2) * J : (t % 2 + 1) * J].indirect(idx6[:]))

        larger = tile("larger", PACK * O, F32)
        for u in range(2):
            nc.vector.tensor_tensor(larger[:, u * 2 * O : (u + 1) * 2 * O], by_idx4[u][:], by_idx5[u][:], ALU.max)
        hid = tile("hid", PACK * O, BF16)
        nc.vector.tensor_tensor(undealt(hid[:], LINE // 4), dealt(larger[:], LINE // 4), dealt(b_g[:], LINE // 4),
                                ALU.subtract)
        hid_w = tile("hid_w", O, U32)
        hid_s = tile("hid_s", O, U8)
        nc.vector.quantize_mx(hid_w[:].bitcast(E5M2), hid_s[:], hid[:])

        tz_g = tile("tz_g", 2 * O, F32, "b_sb1")
        for h in range(2):
            scalar_move(tz_g[:, h * O : (h + 1) * O], tz_sb[:, h * E : (h + 1) * E].indirect(idx7[:]))

        for h in range(2):
            rows = slice(h * P, (h + 1) * P)
            p_ps = psum.tile([P, O], F32, name="p_ps%d" % h)
            nc.tensor.matmul_mx(p_ps[:], lhsT=wb_w[:, rows].bitcast(E2M1), lhsT_scale=wb_s[:, rows],
                                rhs=hid_w[:].bitcast(E5M2), rhs_scale=hid_s[:], start=True, stop=True)
            res = tile("res%d" % h, O, F32)
            nc.vector.tensor_tensor(res[:], p_ps[:], tz_g[:, h * O : (h + 1) * O], ALU.add)
            nc.sync.dma_start(out[rows, :], res[:])
